import numpy as np, ml_dtypes
CORES = [44,45,46,47,172,173,174,175,300,301,302,303,428,429,430,431]
N = 16
import mx_ref
NC, G, KO, SH = 128, 2, 2, 1
C = np.float32(0.023)
BF = ml_dtypes.bfloat16
def cut(t, i, w=512):
    return t[:, w * i:w * i + w]
def tile(rs):
    return np.stack(rs, axis=2).reshape(128, -1).astype(BF)
def layer(w, X):
    out = []
    for i in range(G):
        for t in range(len(X)):
            p = mx_ref.matmul(mx_ref.quantize(cut(w, len(X) * i + t)), X[t])
            z = p if t == 0 else z + p
        out.append(z)
    return out
def act(Z):
    return [np.maximum(s * z, 0) * C for z in Z for s in (1, -1)]
def inputs(rng, e, E):
    def f(*shape):
        v = (rng.standard_normal(shape, dtype=np.float32) * np.exp2(rng.integers(-2, 3, shape[:-1] + (1,)))).astype(BF)
        return mx_ref.spread((v.astype(np.float32) * np.exp2(rng.integers(-E, E + 1, shape[:-2] + (1, 1))).astype(np.float32)).astype(BF), rng, e)
    def packed(k):
        c = np.zeros((N, 128, k * 512), np.uint8); s = np.zeros((N, 128, k * 128), np.uint8)
        for r in range(N):
            for i in range(k):
                a, b = mx_ref.quantize(f(128, 512)); c[r][:, 512 * i:512 * i + 512] = a; s[r][:, 128 * i:128 * i + 128] = mx_ref.plane(b, rng)
        return c, s
    d = {}
    d["kc"], d["ks"] = packed(KO)
    d["x"] = f(N, 128, 4 * NC)
    d["wk"] = f(N, 128, G * 512)
    d["q"] = f(N, 128, 512)
    return d
def setup_inputs(rng):
    return inputs(rng, 0, 0)
def setup_inputs_blocks(rng):
    return inputs(rng, 4, 0)
def setup_inputs_wide(rng):
    return inputs(rng, 0, 8)
def reference(kc, ks, x, wk, q):
    new = [mx_ref.quantize(tile(act(layer(wk[r], [mx_ref.quantize(x[r])])))) for r in range(N)]
    y = np.zeros((N, 128, 128 * KO + NC), np.float32)
    for o in range(N):
        old = (np.ascontiguousarray(kc[o]), mx_ref.live(ks[o]))
        qq = mx_ref.quantize(q[o])
        y[o] = np.concatenate([mx_ref.matmul(qq, old), mx_ref.matmul(qq, new[(o - SH) % N])], axis=1)
    return {"y": y}

from concourse.mybir import dt, AluOpType, ActivationFunctionType

SH = 1
C = 0.023
ENG = 8

SCRATCH = {
    "xb": ("sbuf", [128, 512], "bfloat16"),
    "wb": ("sbuf", [128, 1024], "bfloat16"),
    "qb": ("sbuf", [128, 512], "bfloat16"),
    "kb": ("sbuf", [128, 512], "bfloat16"),
    "xq": ("sbuf", [128, 128], "float8_e4m3fn_x4"),
    "xs": ("sbuf", [128, 128], "uint8"),
    "wq": ("sbuf", [128, 256], "float8_e4m3fn_x4"),
    "ws": ("sbuf", [128, 256], "uint8"),
    "qq": ("sbuf", [128, 128], "float8_e4m3fn_x4"),
    "qs": ("sbuf", [128, 128], "uint8"),
    "mq": ("sbuf", [128, 128], "float8_e4m3fn_x4"),
    "ms": ("sbuf", [128, 128], "uint8"),
    "nq": ("sbuf", [128, 128], "float8_e4m3fn_x4"),
    "ns": ("sbuf", [128, 128], "uint8"),
    "oldq": ("sbuf", [128, 256], "float8_e4m3fn_x4"),
    "olds": ("sbuf", [128, 256], "uint8"),
    "yo": ("sbuf", [128, 256], "float32"),
    "yn": ("sbuf", [128, 128], "float32"),
    "z": ("psum", [128, 1024], "float32"),
    "s": ("psum", [128, 1024], "float32"),
}
SEMAPHORES = ["lx", "lw0", "lw1", "lq", "lk", "ex", "ew0", "ew1", "eq", "z0", "z1", "r", "ek", "so", "sn", "co", "cn",
              "arr", "sent", "sto", "stn"]


def pick(mask, n):
    out = 0
    for b in range(16):
        if n and (mask >> b) & 1:
            out |= 1 << b
            n -= 1
    return out


def rank_program(g, core, T, topo):
    rank = T.rank_of(core)
    if rank is None:
        return
    S = T.sem
    nxt = T.cores[(rank + SH) % len(T.cores)]
    relu = ActivationFunctionType.Relu

    g.sync.dma_start(T.xb[:], T.x[:]).then_inc(S.lx, 16)
    g.sync.dma_start(T.wb[:, 512:1024], T.wk[:, 512:1024]).then_inc(S.lw1, 16)
    g.sync.dma_start(T.qb[:], T.q[:]).then_inc(S.lq, 16)
    g.sync.dma_start(T.oldq[:].bitcast(dt.uint8), T.kc[:]).then_inc(S.lk, 16)
    g.sync.dma_start(T.olds[:], T.ks[:]).then_inc(S.lk, 16)
    g.sync.wait_ge(S.sent, 2 * ENG)
    g.sync.wait_ge(S.co, 1)
    g.sync.dma_start(T.y[:, 0:256], T.yo[:]).then_inc(S.sto, 16)
    g.sync.wait_ge(S.sto, 16)

    g.scalar.dma_start(T.wb[:, 0:512], T.wk[:, 0:512]).then_inc(S.lw0, 16)
    g.scalar.wait_ge(S.z0, 1)
    g.scalar.activation(T.kb[:, 0:512:4], T.z[:, 0:128], relu, scale=C).then_inc(S.r, 1)
    g.scalar.activation(T.kb[:, 1:512:4], T.z[:, 0:128], relu, scale=-C).then_inc(S.r, 1)
    g.scalar.wait_ge(S.so, 1)
    g.scalar.activation(T.yo[:], T.s[:, 0:256], ActivationFunctionType.Copy).then_inc(S.co, 1)
    g.scalar.wait_ge(S.cn, 1)
    g.scalar.dma_start(T.y[:, 256:384], T.yn[:]).then_inc(S.stn, 16)
    g.scalar.wait_ge(S.stn, 16)

    g.vector.wait_ge(S.lx, 16)
    g.vector.quantize_mx(T.xq[:], T.xs[:], T.xb[:]).then_inc(S.ex, 1)
    g.vector.wait_ge(S.lw0, 16)
    g.vector.quantize_mx(T.wq[:, 0:128], T.ws[:, 0:128], T.wb[:, 0:512]).then_inc(S.ew0, 1)
    g.vector.wait_ge(S.lw1, 16)
    g.vector.quantize_mx(T.wq[:, 128:256], T.ws[:, 128:256], T.wb[:, 512:1024]).then_inc(S.ew1, 1)
    g.vector.wait_ge(S.z1, 1)
    g.vector.tensor_scalar(T.kb[:, 2:512:4], T.z[:, 512:640], 0.0, C, AluOpType.max, AluOpType.mult).then_inc(S.r, 1)
    g.vector.tensor_scalar(T.kb[:, 3:512:4], T.z[:, 512:640], -C, 0.0, AluOpType.mult, AluOpType.max).then_inc(S.r, 1)
    g.vector.wait_ge(S.r, 4)
    g.vector.quantize_mx(T.mq[:], T.ms[:], T.kb[:]).then_inc(S.ek, 1)
    g.vector.wait_ge(S.lq, 16)
    g.vector.quantize_mx(T.qq[:], T.qs[:], T.qb[:]).then_inc(S.eq, 1)
    g.vector.wait_ge(S.sn, 1)
    g.vector.tensor_copy(T.yn[:], T.s[:, 512:640]).then_inc(S.cn, 1)

    g.tensor.wait_ge(S.ex, 1)
    g.tensor.wait_ge(S.ew0, 1)
    g.tensor.matmul_mx(T.z[:, 0:128], T.wq[:, 0:128], T.ws[:, 0:128], T.xq[:], T.xs[:], True, True).then_inc(S.z0, 1)
    g.tensor.wait_ge(S.ew1, 1)
    g.tensor.matmul_mx(T.z[:, 512:640], T.wq[:, 128:256], T.ws[:, 128:256], T.xq[:], T.xs[:], True, True).then_inc(S.z1, 1)
    g.tensor.wait_ge(S.eq, 1)
    g.tensor.wait_ge(S.lk, 32)
    g.tensor.matmul_mx(T.s[:, 0:256], T.qq[:], T.qs[:], T.oldq[:], T.olds[:], True, True).then_inc(S.so, 1)
    g.tensor.wait_ge(S.arr, 2 * ENG)
    g.tensor.matmul_mx(T.s[:, 512:640], T.qq[:], T.qs[:], T.nq[:], T.ns[:], True, True).then_inc(S.sn, 1)

    rid, pid = topo.addr(nxt, core)
    m = pick(topo.mask(core, nxt), ENG)
    g.wait_ge(S.ek, 1)
    g.remote_dma(T.nq[:].bitcast(dt.uint8), T.mq[:].bitcast(dt.uint8), S.arr, S.sent, pid, rid, m)
    g.remote_dma(T.ns[:], T.ms[:], S.arr, S.sent, pid, rid, m)
